import numpy as np
import ml_dtypes


def mxq(x, axis, fmt="e4m3"):
    dtype, down = {"e4m3": (ml_dtypes.float8_e4m3fn, 7), "e5m2": (ml_dtypes.float8_e5m2, 14)}[fmt]
    v = np.moveaxis(np.asarray(x, np.float32).astype(ml_dtypes.bfloat16).astype(np.float64), axis, -1)
    blocks = v.reshape(v.shape[:-1] + (-1, 32))
    amax = np.abs(blocks).max(-1, keepdims=True)
    byte = np.maximum(np.where(amax > 0, np.frexp(amax)[1] - 1 + 127, 0) - down, 1)
    scale = np.exp2(byte - 127.0)
    codes = (blocks / scale).astype(np.float32).astype(dtype).astype(np.float64)
    return np.moveaxis((codes * scale).reshape(v.shape), -1, axis)


WIDE = False


def mx_kscale(k):
    if not WIDE:
        return np.ones(k)
    levels = np.array([10, -10, 5, -5, 0])
    if k % 512:
        return np.exp2(np.random.permutation(np.resize(levels, k // 32))).repeat(32)
    a = np.empty((k // 512, 16))
    for p in range(k // 512):
        a[p, :8] = np.random.permutation(np.resize(levels, 8))
        for g in range(8):
            far = levels[np.abs(levels - a[p, g]) >= 10]
            a[p, g + 8] = far[np.random.randint(len(far))]
    return np.exp2(a.ravel()).repeat(32)


BF16 = ml_dtypes.bfloat16


def bf(x):
    return np.asarray(x, np.float32).astype(BF16)


def f64(x):
    return np.asarray(x).astype(np.float64)


M, N, R = 1024, 2048, 512


def _pos(t):
    return np.maximum(t, 0.0)


def _neg(t):
    return np.maximum(-t, 0.0)


def draw0():
    u = mx_kscale(M)
    t = mx_kscale(R)
    return {
        "x": bf(np.random.standard_normal((M, N)) * u[:, None]),
        "f": bf(np.random.standard_normal((M, R)) / np.sqrt(M) * u[:, None]),
        "w": bf(np.random.uniform(0.5, 1.5, M) / (u * u)),
        "g": bf(np.random.uniform(0.2, 1.8, (N, R))),
        "p": bf(np.random.standard_normal(R) * t),
        "q": bf((1.0 + 0.2 * np.random.standard_normal(R)) / t),
    }


def core(x, f, w, g, p, q):
    x, f, w, g, p, q = f64(x), f64(f), f64(w), f64(g), f64(p), f64(q)
    fw = mxq(w[:, None] * f, 0, "e4m3")
    a = mxq(x, 0, "e4m3").T @ fw
    b = q[:, None] * (mxq(f, 0, "e4m3").T @ fw)
    c = mxq(g * p[None, :], 1, "e4m3") @ mxq(b, 0, "e4m3")
    s = np.where(p >= 0, 1.0, -1.0)
    sa = a * s[None, :]
    sc = c * s[None, :]
    num = _pos(sa) + _neg(sc) + 0.5
    den = _neg(sa) + _pos(sc) + 0.5
    return g * np.sqrt(num / den)


def e4m3fn_bytes(y):
    return np.clip(np.asarray(y, np.float64), -448.0, 448.0).astype(np.float32).astype(ml_dtypes.float8_e4m3fn).view(np.uint8)


def e4m3fn_values(b):
    return np.asarray(b, np.uint8).view(ml_dtypes.float8_e4m3fn).astype(np.float64)


def setup_inputs():
    d = draw0()
    x0 = np.asarray(d['x']).astype(np.float64)
    s = (np.max(np.abs(x0), axis=(1,), keepdims=True) / 448.0).astype(np.float32)
    out = {}
    for k, v in d.items():
        if k == 'x':
            out['x_bytes'] = e4m3fn_bytes(x0 / s.astype(np.float64))
            out['x_scale'] = s
        else:
            out[k] = v
    return out


def reference(x_bytes, x_scale, f, w, g, p, q):
    return core(e4m3fn_values(x_bytes) * x_scale.astype(np.float64), f, w, g, p, q)

@@ -1,0 +1,361 @@
+from contextlib import ExitStack
+
+import concourse.mybir as mybir
+from concourse.masks import make_identity
+
+M, N, R = 1024, 2048, 512
+FLOPS = 2 * M * R * N + 2 * M * R * R + 2 * N * R * R
+
+F32 = mybir.dt.float32
+BF16 = mybir.dt.bfloat16
+U32 = mybir.dt.uint32
+U8 = mybir.dt.uint8
+FP8 = mybir.dt.float8_e4m3fn
+FP8X4 = mybir.dt.float8_e4m3fn_x4
+ALU = mybir.AluOpType
+ACT = mybir.ActivationFunctionType
+
+P = 128
+PACK = 4
+K_PASS = P * PACK
+M_PASSES = M // K_PASS
+TILES = N // P
+PAIR = 2 * P
+PAIRS = N // PAIR
+HALF = N // 2
+BATCHES = ((0, 1, 2, 3), (4, 5, 6, 7, 8), (9, 10, 11, 12), (13, 14, 15))
+WIDEN_FIRST = 28
+WIDEN_EACH = 2
+PREP_EACH = 3
+HEAD_PREP = 9
+VECTOR_FINISH = (14, 15)
+LAG = 1
+
+
+def tile_weightedsignedseminmfupdate_kernel(tc, x_bytes, x_scale, f, w, g, p, q, out):
+    nc = tc.nc
+    with ExitStack() as ctx:
+        ctx.enter_context(tc.manual_schedule())
+        keep = ctx.enter_context(tc.tile_pool(name="keep", bufs=1))
+        work = ctx.enter_context(tc.tile_pool(name="work", bufs=3))
+        psum = ctx.enter_context(tc.psum_pool(name="psum", bufs=2))
+
+        zero_row = keep.tile([P, R], BF16, name="zero_row")
+        ones = keep.tile([P, P], BF16, name="ones")
+        nc.vector.memset(zero_row[:], 0.0)
+        nc.scalar.dma_start(out=zero_row[0:1, :], in_=p.unsqueeze(0))
+        nc.vector.memset(ones[:], 1.0)
+        f_raw = []
+        xb = {}
+        g_sb = []
+        x_view = x_bytes.rearrange("(k p t) n -> k p t n", p=P, t=PACK)
+        f_view = f.rearrange("(k p t) r -> k p t r", p=P, t=PACK)
+        g_view = g.rearrange("(c i p) r -> c p i r", i=4, p=P)
+        out_view = out.rearrange("(i p) r -> i p r", p=P)
+        x_sc = keep.tile([P, M_PASSES, PACK], F32, name="x_sc")
+        nc.scalar.dma_start(out=x_sc[:], in_=x_scale.rearrange("(k p t) o -> p k (t o)", p=P, t=PACK))
+        w_sb = keep.tile([P, M_PASSES, PACK], BF16, name="w_sb")
+        nc.scalar.dma_start(out=w_sb[:], in_=w.rearrange("(k p t) -> p k t", p=P, t=PACK))
+        p_sb = keep.tile([P, PACK], BF16, name="p_sb")
+        nc.scalar.dma_start(out=p_sb[:], in_=p.rearrange("(p t) -> p t", t=PACK))
+        q_sb = keep.tile([P, PACK], BF16, name="q_sb")
+        nc.scalar.dma_start(out=q_sb[:], in_=q.rearrange("(p t) -> p t", t=PACK))
+
+        def load_f(k):
+            tl = keep.tile([P, PACK, R], BF16, name=f"f_raw{k}")
+            nc.sync.dma_start(out=tl[:], in_=f_view[k])
+            f_raw.append(tl)
+
+        def load_x(h, k):
+            tl = keep.tile([P, PACK, HALF], U8, name=f"xb{h}{k}")
+            nc.sync.dma_start(out=tl[:], in_=x_view[k][:, :, h * HALF : (h + 1) * HALF])
+            xb[h, k] = tl
+
+        def load_g(c):
+            tl = keep.tile([P, 4, R], BF16, name=f"g_sb{c}")
+            nc.sync.dma_start(out=tl[:], in_=g_view[c])
+            g_sb.append(tl)
+
+        load_x(0, 0)
+        load_f(0)
+        load_f(1)
+        load_x(0, 1)
+        load_g(0)
+        load_x(1, 0)
+        load_g(1)
+        load_x(1, 1)
+        load_g(2)
+        load_g(3)
+
+        warm = keep.tile([P, 1], F32, name="warm")
+        nc.vector.memset(warm[:], 1.0)
+        nc.scalar.activation(out=warm[:], in_=warm[:], func=ACT.Sqrt)
+        ident = keep.tile([P, P], F32, name="ident")
+        make_identity(nc, ident[:])
+        half = keep.tile([P, 1], F32, name="half")
+        nc.gpsimd.memset(half[:], 0.5)
+        s4a = keep.tile([P, PACK], F32, name="s4a")
+        nc.gpsimd.tensor_scalar(out=s4a[:], in0=p_sb[:], scalar1=0.0, scalar2=2.0, op0=ALU.is_ge, op1=ALU.mult)
+        s4 = keep.tile([P, PACK], F32, name="s4")
+        nc.gpsimd.tensor_scalar(out=s4[:], in0=s4a[:], scalar1=-1.0, scalar2=1.0, op0=ALU.add, op1=ALU.mult)
+        qs = keep.tile([P, PACK], F32, name="qs")
+        nc.gpsimd.tensor_tensor(out=qs[:], in0=s4[:], in1=q_sb[:], op=ALU.mult)
+
+        pb = psum.tile([P, R], F32, name="pa", bufs=3)
+        nc.tensor.matmul(pb[:], lhsT=ones[:], rhs=zero_row[:], start=True, stop=True)
+        s2 = keep.tile([P, R], F32, name="s2")
+        nc.vector.tensor_scalar(out=s2[:], in0=pb[:], scalar1=0.0, scalar2=2.0, op0=ALU.is_ge, op1=ALU.mult)
+        s_row = keep.tile([P, R], BF16, name="s_row")
+        nc.vector.tensor_scalar(out=s_row[:], in0=s2[:], scalar1=-1.0, scalar2=None, op0=ALU.add)
+
+        def quantize(src, nm):
+            codes = keep.tile([P, src.shape[1] // PACK], U32, name=nm + "_codes", align_bytes=64)
+            scales = keep.tile([P, src.shape[1] // PACK], U8, name=nm + "_scales", align_bytes=64)
+            nc.vector.quantize_mx(out=codes[:].bitcast(FP8X4), scales=scales[:], in_=src)
+            return codes, scales
+
+        def mx(dst, lhs, lcols, rhs, rcols, start, stop):
+            nc.tensor.matmul_mx(
+                out=dst,
+                lhsT=lhs[0][:, lcols].bitcast(FP8X4),
+                lhsT_scale=lhs[1][:, lcols],
+                rhs=rhs[0][:, rcols].bitcast(FP8X4),
+                rhs_scale=rhs[1][:, rcols],
+                start=start,
+                stop=stop,
+            )
+
+        xw = {}
+        WIDE = N // 4
+
+        def widen(quarter, k, t):
+            if t == 0:
+                tl = keep.tile([P, PACK, WIDE], BF16, name=f"xw{quarter}{k}")
+                xw[quarter, k] = tl
+            src = xb[quarter // 2, k][:, t, (quarter % 2) * WIDE : (quarter % 2 + 1) * WIDE]
+            nc.scalar.activation(out=xw[quarter, k][:, t, :], in_=src.bitcast(FP8), func=ACT.Copy, scale=x_sc[:, k, t : t + 1])
+
+        widen_list = [(h, k, t) for h in range(4) for k in range(2) for t in range(PACK)]
+
+        def widen_some(n):
+            for a in widen_list[:n]:
+                widen(*a)
+            del_n = widen_list[n:]
+            widen_list.clear()
+            widen_list.extend(del_n)
+
+        xi, xq = {}, {}
+
+        def x_interleave(u, k):
+            tl = work.tile([P, PAIR * PACK], BF16, name="xi", bufs=6, align_bytes=64)
+            xi[u, k] = tl
+            cols = slice((u % 2) * PAIR, (u % 2 + 1) * PAIR)
+            nc.vector.tensor_copy(
+                out=tl[:].rearrange("p (n t) -> p n t", t=PACK),
+                in_=xw[u // 2, k][:, :, cols].rearrange("p t n -> p n t"),
+            )
+
+        def x_quantize(u, k):
+            xq[u, k] = quantize(xi[u, k][:], f"x{u}{k}")
+
+        gt, gpi, gpq = {}, {}, {}
+
+        def g_transpose(u):
+            tl = psum.tile([P, 2, PAIR], F32, name="pg", bufs=2)
+            gt[u] = tl
+            for a in range(2):
+                words = g_sb[u // 2][:, 2 * (u % 2) + a, :].bitcast(F32)
+                for e in range(2):
+                    nc.tensor.transpose(tl[:, e, a * P : (a + 1) * P], words[:, e : R // 2 : 2], ident[:])
+
+        def g_load_p(u):
+            tl = work.tile([P, PAIR * PACK], BF16, name="gpi", bufs=2, align_bytes=64)
+            gpi[u] = tl
+            nc.vector.tensor_tensor(
+                out=tl[:].rearrange("p (n u e) -> p n u e", u=2, e=2),
+                in0=gt[u][:].rearrange("p u n -> p (u n)").bitcast(BF16).rearrange("p (u n e) -> p n u e", u=2, e=2),
+                in1=p_sb[:].rearrange("p (u e) -> p u e", e=2).unsqueeze(1).to_broadcast([P, PAIR, 2, 2]),
+                op=ALU.mult,
+            )
+
+        def g_quantize(u):
+            gpq[u] = quantize(gpi[u][:], f"gp{u}")
+
+        prep = []
+        for u in range(PAIRS):
+            prep.append((x_interleave, u, 0))
+            prep.append((x_interleave, u, 1))
+            prep.append((x_quantize, u, 0))
+            prep.append((g_load_p, u))
+            prep.append((x_quantize, u, 1))
+            prep.append((g_quantize, u))
+
+        def prepare(n):
+            for step in prep[:n]:
+                step[0](*step[1:])
+                if step[0] == g_load_p and step[1] + 2 < PAIRS:
+                    g_transpose(step[1] + 2)
+            rest = prep[n:]
+            prep.clear()
+            prep.extend(rest)
+
+        fi, fwi, fq, fwq = [], [], [], []
+
+        def f_interleave(k):
+            tl = work.tile([P, R * PACK], BF16, name="fi", bufs=2, align_bytes=64)
+            fi.append(tl)
+            nc.vector.tensor_tensor(
+                out=tl[:].rearrange("p (j m t) -> p j m t", j=4, t=PACK),
+                in0=f_raw[k][:].rearrange("p t (m j) -> p j m t", j=4),
+                in1=s_row[:].rearrange("p (m j) -> p j m", j=4).unsqueeze(3).to_broadcast([P, 4, P, PACK]),
+                op=ALU.mult,
+            )
+
+        def f_weight(k):
+            tl = work.tile([P, R * PACK], BF16, name="fwi", bufs=2, align_bytes=64)
+            fwi.append(tl)
+            nc.vector.tensor_tensor(
+                out=tl[:].rearrange("p (m j t) -> p m j t", j=4, t=PACK),
+                in0=fi[k][:].rearrange("p (j m t) -> p m j t", j=4, t=PACK),
+                in1=w_sb[:, k, :].unsqueeze(1).unsqueeze(1).to_broadcast([P, P, 4, PACK]),
+                op=ALU.mult,
+            )
+
+        f_interleave(0)
+        f_interleave(1)
+        f_weight(0)
+        fq.append(quantize(fi[0][:], "f0"))
+        f_weight(1)
+        fwq.append(quantize(fwi[0][:], "fw0"))
+        fq.append(quantize(fi[1][:], "f1"))
+        fwq.append(quantize(fwi[1][:], "fw1"))
+
+        widen_some(WIDEN_FIRST)
+
+        g_transpose(0)
+        g_transpose(1)
+        bt = []
+        bi = keep.tile([P, R * PACK], BF16, name="bi", align_bytes=64)
+
+        def gram(j):
+            tl = psum.tile([P, PACK, P], F32, name="pc", bufs=3)
+            bt.append(tl)
+            for t in range(PACK):
+                for k in range(M_PASSES):
+                    mx(tl[:, t, :], fq[k], slice(t * P, (t + 1) * P), fwq[k], slice(j * P, (j + 1) * P), k == 0, k == 1)
+
+        def gram_out(j):
+            nc.vector.tensor_tensor(
+                out=bi[:, j * P * PACK : (j + 1) * P * PACK].rearrange("p (n t) -> p n t", t=PACK),
+                in0=bt[j][:].rearrange("p t n -> p n t"),
+                in1=qs[:].unsqueeze(1).to_broadcast([P, P, PACK]),
+                op=ALU.mult,
+            )
+
+        gram(0)
+        gram(1)
+        gram(2)
+        prepare(1)
+        gram_out(0)
+        gram(3)
+        prepare(1)
+        gram_out(1)
+        prepare(1)
+        gram_out(2)
+        prepare(1)
+        gram_out(3)
+        prepare(1)
+        bq = quantize(bi[:], "b")
+        prepare(HEAD_PREP)
+
+        pa, pc = {}, {}
+
+        def products(i):
+            u, lc = i // 2, slice((i % 2) * P, (i % 2 + 1) * P)
+            full = slice(0, R)
+            tl = psum.tile([P, R], F32, name="pc", bufs=3)
+            pc[i] = tl
+            mx(tl[:], gpq[u], lc, bq, full, True, True)
+            tl = psum.tile([P, R], F32, name="pa", bufs=3)
+            pa[i] = tl
+            for k in range(M_PASSES):
+                mx(tl[:], xq[u, k], lc, fwq[k], full, k == 0, k == M_PASSES - 1)
+
+        cneg, cpos, num, nden = {}, {}, {}, {}
+
+        def parts(i):
+            tl = work.tile([P, R], F32, name="cneg", bufs=3)
+            cneg[i] = tl
+            nc.scalar.activation(out=tl[:], in_=pc[i][:], func=ACT.Relu, scale=-1.0)
+            tl = work.tile([P, R], F32, name="cpos", bufs=3)
+            cpos[i] = tl
+            nc.scalar.activation(out=tl[:], in_=pc[i][:], func=ACT.Relu)
+
+        def sums(i):
+            tl = work.tile([P, R], F32, name="num", bufs=11)
+            num[i] = tl
+            nc.vector.scalar_tensor_tensor(out=tl[:], in0=pa[i][:], scalar=0.0, in1=cneg[i][:], op0=ALU.max, op1=ALU.add)
+            tl = work.tile([P, R], F32, name="nden", bufs=11)
+            nden[i] = tl
+            nc.vector.scalar_tensor_tensor(out=tl[:], in0=pa[i][:], scalar=0.0, in1=cpos[i][:], op0=ALU.min, op1=ALU.subtract)
+
+        def root(i):
+            nc.scalar.activation(out=num[i][:], in_=num[i][:], func=ACT.Sqrt, bias=half[:])
+
+        def inv_root(i):
+            nc.scalar.activation(out=nden[i][:], in_=nden[i][:], func=ACT.Abs_reciprocal_sqrt, scale=-1.0, bias=half[:])
+
+        ratio = {}
+
+        def ratios(i):
+            tl = work.tile([P, R], F32, name="ratio", bufs=4)
+            ratio[i] = tl
+            nc.vector.tensor_tensor(out=tl[:], in0=num[i][:], in1=nden[i][:], op=ALU.mult)
+
+        def finish(i):
+            tl = work.tile([P, R], F32, name="res", bufs=4)
+            eng = nc.vector if i in VECTOR_FINISH else nc.gpsimd
+            eng.tensor_tensor(out=tl[:], in0=ratio[i][:], in1=g_sb[i // 4][:, i % 4, :], op=ALU.mult)
+            nc.sync.dma_start(out=out_view[i], in_=tl[:])
+
+        fns = (root, inv_root)
+        batch_of = {i: b for b, tiles in enumerate(BATCHES) for i in tiles}
+        products(0)
+        products(1)
+        pending, pending_finish = [], []
+        for i in range(TILES):
+            b = batch_of[i]
+            parts(i)
+            widen_some(WIDEN_EACH)
+            if i >= LAG:
+                fns[batch_of[i - LAG] % 2](i - LAG)
+            ready = []
+            if b > 0 and i not in BATCHES[b][:LAG - 1]:
+                prev, cur = BATCHES[b - 1], BATCHES[b][LAG - 1:]
+                pos = cur.index(i)
+                ready = list(prev[pos * len(prev) // len(cur) : (pos + 1) * len(prev) // len(cur)])
+                for j in ready:
+                    fns[b % 2](j)
+            sums(i)
+            for j in pending_finish:
+                finish(j)
+            pending_finish = list(pending)
+            for j in pending:
+                ratios(j)
+            prepare(PREP_EACH)
+            if i + 2 < TILES:
+                products(i + 2)
+            pending = ready
+        last = BATCHES[-1]
+        for i in range(TILES - LAG, TILES):
+            fns[batch_of[i] % 2](i)
+        for j in pending_finish:
+            finish(j)
+        for j in pending:
+            ratios(j)
+            finish(j)
+        for j in last:
+            fns[len(BATCHES) % 2](j)
+        for j in last:
+            ratios(j)
+            finish(j)

@@ -22,14 +22,13 @@ M_PASSES = M // K_PASS
 TILES = N // P
 PAIR = 2 * P
 PAIRS = N // PAIR
-HALF = N // 2
-BATCHES = ((0, 1, 2, 3), (4, 5, 6, 7, 8), (9, 10, 11, 12), (13, 14, 15))
-WIDEN_FIRST = 28
-WIDEN_EACH = 2
-PREP_EACH = 3
-HEAD_PREP = 9
-VECTOR_FINISH = (14, 15)
-LAG = 1
+WIDE = N // 4
+BATCHES = ((0, 1), (2, 3, 4), (5, 6), (7,))
+WIDEN_FIRST = 24
+WIDEN_EACH = 3
+VECTOR_FINISH = (6, 7)
+PE_MIX = ()
+NBUF = 5
 
 
 def tile_weightedsignedseminmfupdate_kernel(tc, x_bytes, x_scale, f, w, g, p, q, out):
@@ -38,7 +37,7 @@ def tile_weightedsignedseminmfupdate_kernel(tc, x_bytes, x_scale, f, w, g, p, q,
         ctx.enter_context(tc.manual_schedule())
         keep = ctx.enter_context(tc.tile_pool(name="keep", bufs=1))
         work = ctx.enter_context(tc.tile_pool(name="work", bufs=3))
-        psum = ctx.enter_context(tc.psum_pool(name="psum", bufs=2))
+        psum = ctx.enter_context(tc.psum_pool(name="psum", bufs=1))
 
         zero_row = keep.tile([P, R], BF16, name="zero_row")
         ones = keep.tile([P, P], BF16, name="ones")
@@ -51,7 +50,7 @@ def tile_weightedsignedseminmfupdate_kernel(tc, x_bytes, x_scale, f, w, g, p, q,
         x_view = x_bytes.rearrange("(k p t) n -> k p t n", p=P, t=PACK)
         f_view = f.rearrange("(k p t) r -> k p t r", p=P, t=PACK)
         g_view = g.rearrange("(c i p) r -> c p i r", i=4, p=P)
-        out_view = out.rearrange("(i p) r -> i p r", p=P)
+        out_view = out.rearrange("(u i p) r -> u p i r", i=2, p=P)
         x_sc = keep.tile([P, M_PASSES, PACK], F32, name="x_sc")
         nc.scalar.dma_start(out=x_sc[:], in_=x_scale.rearrange("(k p t) o -> p k (t o)", p=P, t=PACK))
         w_sb = keep.tile([P, M_PASSES, PACK], BF16, name="w_sb")
@@ -62,13 +61,13 @@ def tile_weightedsignedseminmfupdate_kernel(tc, x_bytes, x_scale, f, w, g, p, q,
         nc.scalar.dma_start(out=q_sb[:], in_=q.rearrange("(p t) -> p t", t=PACK))
 
         def load_f(k):
-            tl = keep.tile([P, PACK, R], BF16, name=f"f_raw{k}")
+            tl = work.tile([P, PACK, R], BF16, name=f"f_raw{k}", tag="big", bufs=16, align_bytes=64)
             nc.sync.dma_start(out=tl[:], in_=f_view[k])
             f_raw.append(tl)
 
         def load_x(h, k):
-            tl = keep.tile([P, PACK, HALF], U8, name=f"xb{h}{k}")
-            nc.sync.dma_start(out=tl[:], in_=x_view[k][:, :, h * HALF : (h + 1) * HALF])
+            tl = keep.tile([P, PACK, WIDE], U8, name=f"xb{h}{k}")
+            nc.sync.dma_start(out=tl[:], in_=x_view[k][:, :, h * WIDE : (h + 1) * WIDE])
             xb[h, k] = tl
 
         def load_g(c):
@@ -82,9 +81,13 @@ def tile_weightedsignedseminmfupdate_kernel(tc, x_bytes, x_scale, f, w, g, p, q,
         load_x(0, 1)
         load_g(0)
         load_x(1, 0)
-        load_g(1)
         load_x(1, 1)
+        load_g(1)
+        load_x(2, 0)
+        load_x(2, 1)
         load_g(2)
+        load_x(3, 0)
+        load_x(3, 1)
         load_g(3)
 
         warm = keep.tile([P, 1], F32, name="warm")
@@ -100,13 +103,15 @@ def tile_weightedsignedseminmfupdate_kernel(tc, x_bytes, x_scale, f, w, g, p, q,
         nc.gpsimd.tensor_scalar(out=s4[:], in0=s4a[:], scalar1=-1.0, scalar2=1.0, op0=ALU.add, op1=ALU.mult)
         qs = keep.tile([P, PACK], F32, name="qs")
         nc.gpsimd.tensor_tensor(out=qs[:], in0=s4[:], in1=q_sb[:], op=ALU.mult)
+        ident_b = keep.tile([P, P], BF16, name="ident_b")
+        nc.gpsimd.tensor_copy(out=ident_b[:], in_=ident[:])
 
-        pb = psum.tile([P, R], F32, name="pa", bufs=3)
+        pb = psum.tile([P, R], F32, name="pa", bufs=2)
         nc.tensor.matmul(pb[:], lhsT=ones[:], rhs=zero_row[:], start=True, stop=True)
         s2 = keep.tile([P, R], F32, name="s2")
-        nc.vector.tensor_scalar(out=s2[:], in0=pb[:], scalar1=0.0, scalar2=2.0, op0=ALU.is_ge, op1=ALU.mult)
+        nc.vector.tensor_scalar(out=s2[:], in0=pb[:], scalar1=0.0, scalar2=-2.0, op0=ALU.is_ge, op1=ALU.mult)
         s_row = keep.tile([P, R], BF16, name="s_row")
-        nc.vector.tensor_scalar(out=s_row[:], in0=s2[:], scalar1=-1.0, scalar2=None, op0=ALU.add)
+        nc.vector.tensor_scalar(out=s_row[:], in0=s2[:], scalar1=1.0, scalar2=None, op0=ALU.add)
 
         def quantize(src, nm):
             codes = keep.tile([P, src.shape[1] // PACK], U32, name=nm + "_codes", align_bytes=64)
@@ -126,25 +131,43 @@ def tile_weightedsignedseminmfupdate_kernel(tc, x_bytes, x_scale, f, w, g, p, q,
             )
 
         xw = {}
-        WIDE = N // 4
 
-        def widen(quarter, k, t):
+        def widen(h, k, t):
             if t == 0:
-                tl = keep.tile([P, PACK, WIDE], BF16, name=f"xw{quarter}{k}")
-                xw[quarter, k] = tl
-            src = xb[quarter // 2, k][:, t, (quarter % 2) * WIDE : (quarter % 2 + 1) * WIDE]
-            nc.scalar.activation(out=xw[quarter, k][:, t, :], in_=src.bitcast(FP8), func=ACT.Copy, scale=x_sc[:, k, t : t + 1])
+                tl = keep.tile([P, PACK, WIDE], BF16, name=f"xw{h}{k}")
+                xw[h, k] = tl
+            nc.scalar.activation(
+                out=xw[h, k][:, t, :], in_=xb[h, k][:, t, :].bitcast(FP8), func=ACT.Copy, scale=x_sc[:, k, t : t + 1]
+            )
 
         widen_list = [(h, k, t) for h in range(4) for k in range(2) for t in range(PACK)]
 
         def widen_some(n):
             for a in widen_list[:n]:
                 widen(*a)
-            del_n = widen_list[n:]
+            rest = widen_list[n:]
             widen_list.clear()
-            widen_list.extend(del_n)
+            widen_list.extend(rest)
 
-        xi, xq = {}, {}
+        xi, xq, px = {}, {}, {}
+
+        def x_mix(u, k):
+            tl = psum.tile([P, PAIR, PACK], BF16, name="px", bufs=1)
+            px[u, k] = tl
+            for a in range(2):
+                c0 = (u % 2) * PAIR + a * P
+                nc.tensor.matmul(
+                    tl[:, a * P : (a + 1) * P, :],
+                    lhsT=ident_b[:],
+                    rhs=xw[u // 2, k][:, :, c0 : c0 + P].rearrange("p t n -> p n t"),
+                    start=True,
+                    stop=True,
+                )
+
+        def x_out(u, k):
+            tl = work.tile([P, PAIR * PACK], BF16, name="xi", bufs=6, align_bytes=64)
+            xi[u, k] = tl
+            nc.scalar.copy(out=tl[:], in_=px[u, k][:].rearrange("p n t -> p (n t)"))
 
         def x_interleave(u, k):
             tl = work.tile([P, PAIR * PACK], BF16, name="xi", bufs=6, align_bytes=64)
@@ -161,7 +184,7 @@ def tile_weightedsignedseminmfupdate_kernel(tc, x_bytes, x_scale, f, w, g, p, q,
         gt, gpi, gpq = {}, {}, {}
 
         def g_transpose(u):
-            tl = psum.tile([P, 2, PAIR], F32, name="pg", bufs=2)
+            tl = psum.tile([P, 2, PAIR], F32, name="pg", bufs=1)
             gt[u] = tl
             for a in range(2):
                 words = g_sb[u // 2][:, 2 * (u % 2) + a, :].bitcast(F32)
@@ -169,7 +192,7 @@ def tile_weightedsignedseminmfupdate_kernel(tc, x_bytes, x_scale, f, w, g, p, q,
                     nc.tensor.transpose(tl[:, e, a * P : (a + 1) * P], words[:, e : R // 2 : 2], ident[:])
 
         def g_load_p(u):
-            tl = work.tile([P, PAIR * PACK], BF16, name="gpi", bufs=2, align_bytes=64)
+            tl = work.tile([P, PAIR * PACK], BF16, name="gpi", bufs=3, align_bytes=64)
             gpi[u] = tl
             nc.vector.tensor_tensor(
                 out=tl[:].rearrange("p (n u e) -> p n u e", u=2, e=2),
@@ -181,28 +204,10 @@ def tile_weightedsignedseminmfupdate_kernel(tc, x_bytes, x_scale, f, w, g, p, q,
         def g_quantize(u):
             gpq[u] = quantize(gpi[u][:], f"gp{u}")
 
-        prep = []
-        for u in range(PAIRS):
-            prep.append((x_interleave, u, 0))
-            prep.append((x_interleave, u, 1))
-            prep.append((x_quantize, u, 0))
-            prep.append((g_load_p, u))
-            prep.append((x_quantize, u, 1))
-            prep.append((g_quantize, u))
-
-        def prepare(n):
-            for step in prep[:n]:
-                step[0](*step[1:])
-                if step[0] == g_load_p and step[1] + 2 < PAIRS:
-                    g_transpose(step[1] + 2)
-            rest = prep[n:]
-            prep.clear()
-            prep.extend(rest)
-
         fi, fwi, fq, fwq = [], [], [], []
 
         def f_interleave(k):
-            tl = work.tile([P, R * PACK], BF16, name="fi", bufs=2, align_bytes=64)
+            tl = work.tile([P, R * PACK], BF16, name="fi", tag="big", bufs=16, align_bytes=64)
             fi.append(tl)
             nc.vector.tensor_tensor(
                 out=tl[:].rearrange("p (j m t) -> p j m t", j=4, t=PACK),
@@ -212,7 +217,7 @@ def tile_weightedsignedseminmfupdate_kernel(tc, x_bytes, x_scale, f, w, g, p, q,
             )
 
         def f_weight(k):
-            tl = work.tile([P, R * PACK], BF16, name="fwi", bufs=2, align_bytes=64)
+            tl = work.tile([P, R * PACK], BF16, name="fwi", tag="big", bufs=16, align_bytes=64)
             fwi.append(tl)
             nc.vector.tensor_tensor(
                 out=tl[:].rearrange("p (m j t) -> p m j t", j=4, t=PACK),
@@ -230,15 +235,12 @@ def tile_weightedsignedseminmfupdate_kernel(tc, x_bytes, x_scale, f, w, g, p, q,
         fq.append(quantize(fi[1][:], "f1"))
         fwq.append(quantize(fwi[1][:], "fw1"))
 
-        widen_some(WIDEN_FIRST)
-
-        g_transpose(0)
-        g_transpose(1)
         bt = []
         bi = keep.tile([P, R * PACK], BF16, name="bi", align_bytes=64)
+        GRAM_BANKS = ("pc", "pu", "pc", "pu")
 
         def gram(j):
-            tl = psum.tile([P, PACK, P], F32, name="pc", bufs=3)
+            tl = psum.tile([P, PACK, P], F32, name=GRAM_BANKS[j], bufs=2)
             bt.append(tl)
             for t in range(PACK):
                 for k in range(M_PASSES):
@@ -252,110 +254,155 @@ def tile_weightedsignedseminmfupdate_kernel(tc, x_bytes, x_scale, f, w, g, p, q,
                 op=ALU.mult,
             )
 
-        gram(0)
-        gram(1)
-        gram(2)
-        prepare(1)
+        mixed = [(u, 0) for u in range(PAIRS)] + list(PE_MIX)
+
+        widen_some(4)
+        x_mix(0, 0)
+        widen_some(4)
+        x_out(0, 0)
+        x_mix(1, 0)
+        g_transpose(0)
+        widen_some(4)
+        x_out(1, 0)
+        x_mix(2, 0)
+        widen_some(WIDEN_FIRST - 12)
+        for j in range(4):
+            gram(j)
+        x_interleave(0, 1)
+        x_interleave(1, 1)
+        g_load_p(0)
+        g_transpose(1)
+        x_quantize(0, 0)
         gram_out(0)
-        gram(3)
-        prepare(1)
         gram_out(1)
-        prepare(1)
+        x_quantize(0, 1)
         gram_out(2)
-        prepare(1)
+        g_quantize(0)
         gram_out(3)
-        prepare(1)
+        g_load_p(1)
+        g_transpose(2)
         bq = quantize(bi[:], "b")
-        prepare(HEAD_PREP)
+        x_quantize(1, 0)
+        x_quantize(1, 1)
+        g_quantize(1)
 
-        pa, pc = {}, {}
+        pa, pc, pu = {}, {}, {}
+        full = slice(0, R)
 
-        def products(i):
-            u, lc = i // 2, slice((i % 2) * P, (i % 2 + 1) * P)
-            full = slice(0, R)
-            tl = psum.tile([P, R], F32, name="pc", bufs=3)
-            pc[i] = tl
-            mx(tl[:], gpq[u], lc, bq, full, True, True)
-            tl = psum.tile([P, R], F32, name="pa", bufs=3)
-            pa[i] = tl
-            for k in range(M_PASSES):
-                mx(tl[:], xq[u, k], lc, fwq[k], full, k == 0, k == M_PASSES - 1)
+        def cols_of(i):
+            return slice((i % 2) * P, (i % 2 + 1) * P)
 
-        cneg, cpos, num, nden = {}, {}, {}, {}
+        def products(u):
+            for i in (2 * u, 2 * u + 1):
+                tl = psum.tile([P, R], F32, name="pc", bufs=2)
+                pc[i] = tl
+                mx(tl[:], gpq[u], cols_of(i), bq, full, True, True)
+            for i in (2 * u, 2 * u + 1):
+                tl = psum.tile([P, R], F32, name="pa", bufs=2)
+                pa[i] = tl
+                for k in range(M_PASSES):
+                    mx(tl[:], xq[u, k], cols_of(i), fwq[k], full, k == 0, k == M_PASSES - 1)
+            for i in (2 * u, 2 * u + 1):
+                tl = psum.tile([P, R], F32, name="pu", bufs=2)
+                pu[i] = tl
+                for k in range(M_PASSES):
+                    mx(tl[:], xq[u, k], cols_of(i), fwq[k], full, k == 0, False)
+                mx(tl[:], gpq[u], cols_of(i), bq, full, False, True)
 
-        def parts(i):
-            tl = work.tile([P, R], F32, name="cneg", bufs=3)
-            cneg[i] = tl
-            nc.scalar.activation(out=tl[:], in_=pc[i][:], func=ACT.Relu, scale=-1.0)
-            tl = work.tile([P, R], F32, name="cpos", bufs=3)
-            cpos[i] = tl
-            nc.scalar.activation(out=tl[:], in_=pc[i][:], func=ACT.Relu)
+        cneg, num, den = {}, {}, {}
 
-        def sums(i):
-            tl = work.tile([P, R], F32, name="num", bufs=11)
-            num[i] = tl
-            nc.vector.scalar_tensor_tensor(out=tl[:], in0=pa[i][:], scalar=0.0, in1=cneg[i][:], op0=ALU.max, op1=ALU.add)
-            tl = work.tile([P, R], F32, name="nden", bufs=11)
-            nden[i] = tl
-            nc.vector.scalar_tensor_tensor(out=tl[:], in0=pa[i][:], scalar=0.0, in1=cpos[i][:], op0=ALU.min, op1=ALU.subtract)
+        def parts(u):
+            tl = work.tile([P, 2, R], F32, name="cneg", bufs=2)
+            cneg[u] = tl
+            for a in range(2):
+                nc.scalar.activation(out=tl[:, a, :], in_=pc[2 * u + a][:], func=ACT.Relu, scale=-1.0)
 
-        def root(i):
-            nc.scalar.activation(out=num[i][:], in_=num[i][:], func=ACT.Sqrt, bias=half[:])
+        def sum_num(u):
+            tl = work.tile([P, 2, R], F32, name="num", tag="big", bufs=16, align_bytes=64)
+            num[u] = tl
+            for a in range(2):
+                nc.vector.scalar_tensor_tensor(
+                    out=tl[:, a, :], in0=pa[2 * u + a][:], scalar=0.0, in1=cneg[u][:, a, :], op0=ALU.min, op1=ALU.subtract
+                )
 
-        def inv_root(i):
-            nc.scalar.activation(out=nden[i][:], in_=nden[i][:], func=ACT.Abs_reciprocal_sqrt, scale=-1.0, bias=half[:])
+        def sum_den(u):
+            tl = work.tile([P, 2, R], F32, name="den", tag="big", bufs=16, align_bytes=64)
+            den[u] = tl
+            for a in range(2):
+                nc.vector.tensor_tensor(out=tl[:, a, :], in0=pu[2 * u + a][:], in1=num[u][:, a, :], op=ALU.subtract)
 
-        ratio = {}
+        def root(u, s):
+            nc.scalar.activation(out=num[u][:, s, :], in_=num[u][:, s, :], func=ACT.Sqrt, scale=-1.0, bias=half[:])
 
-        def ratios(i):
-            tl = work.tile([P, R], F32, name="ratio", bufs=4)
-            ratio[i] = tl
-            nc.vector.tensor_tensor(out=tl[:], in0=num[i][:], in1=nden[i][:], op=ALU.mult)
+        def inv_root(u, s):
+            nc.scalar.activation(out=den[u][:, s, :], in_=den[u][:, s, :], func=ACT.Abs_reciprocal_sqrt, bias=half[:])
 
-        def finish(i):
-            tl = work.tile([P, R], F32, name="res", bufs=4)
-            eng = nc.vector if i in VECTOR_FINISH else nc.gpsimd
-            eng.tensor_tensor(out=tl[:], in0=ratio[i][:], in1=g_sb[i // 4][:, i % 4, :], op=ALU.mult)
-            nc.sync.dma_start(out=out_view[i], in_=tl[:])
+        ratio, res = {}, {}
+        both = slice(0, 2)
+
+        def ratios(u, s):
+            if u not in ratio:
+                tl = work.tile([P, 2, R], F32, name="ratio", bufs=2)
+                ratio[u] = tl
+            nc.vector.tensor_tensor(out=ratio[u][:, s, :], in0=num[u][:, s, :], in1=den[u][:, s, :], op=ALU.mult)
+
+        def finish(u, s):
+            if u not in res:
+                tl = work.tile([P, 2, R], F32, name="res", bufs=3)
+                res[u] = tl
+            eng = nc.vector if u in VECTOR_FINISH else nc.gpsimd
+            gs = g_sb[u // 2][:, 2 * (u % 2) : 2 * (u % 2) + 2, :]
+            eng.tensor_tensor(out=res[u][:, s, :], in0=ratio[u][:, s, :], in1=gs[:, s, :], op=ALU.mult)
+            nc.sync.dma_start(out=out_view[u][:, s, :], in_=res[u][:, s, :])
 
         fns = (root, inv_root)
-        batch_of = {i: b for b, tiles in enumerate(BATCHES) for i in tiles}
+        batch_of = {u: b for b, us in enumerate(BATCHES) for u in us}
         products(0)
-        products(1)
-        pending, pending_finish = [], []
-        for i in range(TILES):
-            b = batch_of[i]
-            parts(i)
+        parts(0)
+        queue = []
+        for u in range(PAIRS):
+            b = batch_of[u]
+            v = u + 2
+            prep = v < PAIRS
+            ready = list(queue)
+            queue.clear()
+            sum_num(u)
+            if prep:
+                g_load_p(v)
+            sum_den(u)
+            if u + 1 < PAIRS:
+                products(u + 1)
+            if prep:
+                x_out(v, 0)
+            if v + 1 < PAIRS:
+                x_mix(v + 1, 0)
+                g_transpose(v + 1)
+            if u + 1 < PAIRS:
+                parts(u + 1)
             widen_some(WIDEN_EACH)
-            if i >= LAG:
-                fns[batch_of[i - LAG] % 2](i - LAG)
-            ready = []
-            if b > 0 and i not in BATCHES[b][:LAG - 1]:
-                prev, cur = BATCHES[b - 1], BATCHES[b][LAG - 1:]
-                pos = cur.index(i)
-                ready = list(prev[pos * len(prev) // len(cur) : (pos + 1) * len(prev) // len(cur)])
-                for j in ready:
-                    fns[b % 2](j)
-            sums(i)
-            for j in pending_finish:
-                finish(j)
-            pending_finish = list(pending)
-            for j in pending:
-                ratios(j)
-            prepare(PREP_EACH)
-            if i + 2 < TILES:
-                products(i + 2)
-            pending = ready
-        last = BATCHES[-1]
-        for i in range(TILES - LAG, TILES):
-            fns[batch_of[i] % 2](i)
-        for j in pending_finish:
-            finish(j)
-        for j in pending:
-            ratios(j)
-            finish(j)
-        for j in last:
-            fns[len(BATCHES) % 2](j)
-        for j in last:
-            ratios(j)
-            finish(j)
+            fns[b % 2](u, both)
+            if b > 0:
+                prev, cur = BATCHES[b - 1], BATCHES[b]
+                pos = cur.index(u)
+                for j in prev[pos * len(prev) // len(cur) : (pos + 1) * len(prev) // len(cur)]:
+                    fns[b % 2](j, both)
+                    queue.append(j)
+            if prep:
+                if (v, 1) not in mixed:
+                    x_interleave(v, 1)
+                x_quantize(v, 0)
+                x_quantize(v, 1)
+                g_quantize(v)
+            for j in ready:
+                ratios(j, both)
+                finish(j, both)
+        for j in queue:
+            ratios(j, both)
+            finish(j, both)
+        for j in BATCHES[-1]:
+            for a in range(2):
+                fns[len(BATCHES) % 2](j, slice(a, a + 1))
+            for a in range(2):
+                ratios(j, slice(a, a + 1))
+            for a in range(2):
+                finish(j, slice(a, a + 1))

from contextlib import ExitStack

import concourse.mybir as mybir
from concourse.masks import make_identity

M, N, R = 1024, 2048, 512
FLOPS = 2 * M * R * N + 2 * M * R * R + 2 * N * R * R

F32 = mybir.dt.float32
BF16 = mybir.dt.bfloat16
U32 = mybir.dt.uint32
U8 = mybir.dt.uint8
FP8 = mybir.dt.float8_e4m3fn
FP8X4 = mybir.dt.float8_e4m3fn_x4
ALU = mybir.AluOpType
ACT = mybir.ActivationFunctionType

P = 128
PACK = 4
K_PASS = P * PACK
M_PASSES = M // K_PASS
TILES = N // P
PAIR = 2 * P
PAIRS = N // PAIR
WIDE = N // 4
BATCHES = ((0, 1), (2, 3, 4), (5, 6), (7,))
WIDEN_FIRST = 24
WIDEN_EACH = 3
VECTOR_FINISH = (6, 7)
PE_MIX = ()
NBUF = 5


def tile_weightedsignedseminmfupdate_kernel(tc, x_bytes, x_scale, f, w, g, p, q, out):
    nc = tc.nc
    with ExitStack() as ctx:
        ctx.enter_context(tc.manual_schedule())
        keep = ctx.enter_context(tc.tile_pool(name="keep", bufs=1))
        work = ctx.enter_context(tc.tile_pool(name="work", bufs=3))
        psum = ctx.enter_context(tc.psum_pool(name="psum", bufs=1))

        zero_row = keep.tile([P, R], BF16, name="zero_row")
        ones = keep.tile([P, P], BF16, name="ones")
        nc.vector.memset(zero_row[:], 0.0)
        nc.scalar.dma_start(out=zero_row[0:1, :], in_=p.unsqueeze(0))
        nc.vector.memset(ones[:], 1.0)
        f_raw = []
        xb = {}
        g_sb = []
        x_view = x_bytes.rearrange("(k p t) n -> k p t n", p=P, t=PACK)
        f_view = f.rearrange("(k p t) r -> k p t r", p=P, t=PACK)
        g_view = g.rearrange("(c i p) r -> c p i r", i=4, p=P)
        out_view = out.rearrange("(u i p) r -> u p i r", i=2, p=P)
        x_sc = keep.tile([P, M_PASSES, PACK], F32, name="x_sc")
        nc.scalar.dma_start(out=x_sc[:], in_=x_scale.rearrange("(k p t) o -> p k (t o)", p=P, t=PACK))
        w_sb = keep.tile([P, M_PASSES, PACK], BF16, name="w_sb")
        nc.scalar.dma_start(out=w_sb[:], in_=w.rearrange("(k p t) -> p k t", p=P, t=PACK))
        p_sb = keep.tile([P, PACK], BF16, name="p_sb")
        nc.scalar.dma_start(out=p_sb[:], in_=p.rearrange("(p t) -> p t", t=PACK))
        q_sb = keep.tile([P, PACK], BF16, name="q_sb")
        nc.scalar.dma_start(out=q_sb[:], in_=q.rearrange("(p t) -> p t", t=PACK))

        def load_f(k):
            tl = work.tile([P, PACK, R], BF16, name=f"f_raw{k}", tag="big", bufs=16, align_bytes=64)
            nc.sync.dma_start(out=tl[:], in_=f_view[k])
            f_raw.append(tl)

        def load_x(h, k):
            tl = keep.tile([P, PACK, WIDE], U8, name=f"xb{h}{k}")
            nc.sync.dma_start(out=tl[:], in_=x_view[k][:, :, h * WIDE : (h + 1) * WIDE])
            xb[h, k] = tl

        def load_g(c):
            tl = keep.tile([P, 4, R], BF16, name=f"g_sb{c}")
            nc.sync.dma_start(out=tl[:], in_=g_view[c])
            g_sb.append(tl)

        load_x(0, 0)
        load_f(0)
        load_f(1)
        load_x(0, 1)
        load_g(0)
        load_x(1, 0)
        load_x(1, 1)
        load_g(1)
        load_x(2, 0)
        load_x(2, 1)
        load_g(2)
        load_x(3, 0)
        load_x(3, 1)
        load_g(3)

        warm = keep.tile([P, 1], F32, name="warm")
        nc.vector.memset(warm[:], 1.0)
        nc.scalar.activation(out=warm[:], in_=warm[:], func=ACT.Sqrt)
        ident = keep.tile([P, P], F32, name="ident")
        make_identity(nc, ident[:])
        half = keep.tile([P, 1], F32, name="half")
        nc.gpsimd.memset(half[:], 0.5)
        s4a = keep.tile([P, PACK], F32, name="s4a")
        nc.gpsimd.tensor_scalar(out=s4a[:], in0=p_sb[:], scalar1=0.0, scalar2=2.0, op0=ALU.is_ge, op1=ALU.mult)
        s4 = keep.tile([P, PACK], F32, name="s4")
        nc.gpsimd.tensor_scalar(out=s4[:], in0=s4a[:], scalar1=-1.0, scalar2=1.0, op0=ALU.add, op1=ALU.mult)
        qs = keep.tile([P, PACK], F32, name="qs")
        nc.gpsimd.tensor_tensor(out=qs[:], in0=s4[:], in1=q_sb[:], op=ALU.mult)
        ident_b = keep.tile([P, P], BF16, name="ident_b")
        nc.gpsimd.tensor_copy(out=ident_b[:], in_=ident[:])

        pb = psum.tile([P, R], F32, name="pa", bufs=2)
        nc.tensor.matmul(pb[:], lhsT=ones[:], rhs=zero_row[:], start=True, stop=True)
        s2 = keep.tile([P, R], F32, name="s2")
        nc.vector.tensor_scalar(out=s2[:], in0=pb[:], scalar1=0.0, scalar2=-2.0, op0=ALU.is_ge, op1=ALU.mult)
        s_row = keep.tile([P, R], BF16, name="s_row")
        nc.vector.tensor_scalar(out=s_row[:], in0=s2[:], scalar1=1.0, scalar2=None, op0=ALU.add)

        def quantize(src, nm):
            codes = keep.tile([P, src.shape[1] // PACK], U32, name=nm + "_codes", align_bytes=64)
            scales = keep.tile([P, src.shape[1] // PACK], U8, name=nm + "_scales", align_bytes=64)
            nc.vector.quantize_mx(out=codes[:].bitcast(FP8X4), scales=scales[:], in_=src)
            return codes, scales

        def mx(dst, lhs, lcols, rhs, rcols, start, stop):
            nc.tensor.matmul_mx(
                out=dst,
                lhsT=lhs[0][:, lcols].bitcast(FP8X4),
                lhsT_scale=lhs[1][:, lcols],
                rhs=rhs[0][:, rcols].bitcast(FP8X4),
                rhs_scale=rhs[1][:, rcols],
                start=start,
                stop=stop,
            )

        xw = {}

        def widen(h, k, t):
            if t == 0:
                tl = keep.tile([P, PACK, WIDE], BF16, name=f"xw{h}{k}")
                xw[h, k] = tl
            nc.scalar.activation(
                out=xw[h, k][:, t, :], in_=xb[h, k][:, t, :].bitcast(FP8), func=ACT.Copy, scale=x_sc[:, k, t : t + 1]
            )

        widen_list = [(h, k, t) for h in range(4) for k in range(2) for t in range(PACK)]

        def widen_some(n):
            for a in widen_list[:n]:
                widen(*a)
            rest = widen_list[n:]
            widen_list.clear()
            widen_list.extend(rest)

        xi, xq, px = {}, {}, {}

        def x_mix(u, k):
            tl = psum.tile([P, PAIR, PACK], BF16, name="px", bufs=1)
            px[u, k] = tl
            for a in range(2):
                c0 = (u % 2) * PAIR + a * P
                nc.tensor.matmul(
                    tl[:, a * P : (a + 1) * P, :],
                    lhsT=ident_b[:],
                    rhs=xw[u // 2, k][:, :, c0 : c0 + P].rearrange("p t n -> p n t"),
                    start=True,
                    stop=True,
                )

        def x_out(u, k):
            tl = work.tile([P, PAIR * PACK], BF16, name="xi", bufs=6, align_bytes=64)
            xi[u, k] = tl
            nc.scalar.copy(out=tl[:], in_=px[u, k][:].rearrange("p n t -> p (n t)"))

        def x_interleave(u, k):
            tl = work.tile([P, PAIR * PACK], BF16, name="xi", bufs=6, align_bytes=64)
            xi[u, k] = tl
            cols = slice((u % 2) * PAIR, (u % 2 + 1) * PAIR)
            nc.vector.tensor_copy(
                out=tl[:].rearrange("p (n t) -> p n t", t=PACK),
                in_=xw[u // 2, k][:, :, cols].rearrange("p t n -> p n t"),
            )

        def x_quantize(u, k):
            xq[u, k] = quantize(xi[u, k][:], f"x{u}{k}")

        gt, gpi, gpq = {}, {}, {}

        def g_transpose(u):
            tl = psum.tile([P, 2, PAIR], F32, name="pg", bufs=1)
            gt[u] = tl
            for a in range(2):
                words = g_sb[u // 2][:, 2 * (u % 2) + a, :].bitcast(F32)
                for e in range(2):
                    nc.tensor.transpose(tl[:, e, a * P : (a + 1) * P], words[:, e : R // 2 : 2], ident[:])

        def g_load_p(u):
            tl = work.tile([P, PAIR * PACK], BF16, name="gpi", bufs=3, align_bytes=64)
            gpi[u] = tl
            nc.vector.tensor_tensor(
                out=tl[:].rearrange("p (n u e) -> p n u e", u=2, e=2),
                in0=gt[u][:].rearrange("p u n -> p (u n)").bitcast(BF16).rearrange("p (u n e) -> p n u e", u=2, e=2),
                in1=p_sb[:].rearrange("p (u e) -> p u e", e=2).unsqueeze(1).to_broadcast([P, PAIR, 2, 2]),
                op=ALU.mult,
            )

        def g_quantize(u):
            gpq[u] = quantize(gpi[u][:], f"gp{u}")

        fi, fwi, fq, fwq = [], [], [], []

        def f_interleave(k):
            tl = work.tile([P, R * PACK], BF16, name="fi", tag="big", bufs=16, align_bytes=64)
            fi.append(tl)
            nc.vector.tensor_tensor(
                out=tl[:].rearrange("p (j m t) -> p j m t", j=4, t=PACK),
                in0=f_raw[k][:].rearrange("p t (m j) -> p j m t", j=4),
                in1=s_row[:].rearrange("p (m j) -> p j m", j=4).unsqueeze(3).to_broadcast([P, 4, P, PACK]),
                op=ALU.mult,
            )

        def f_weight(k):
            tl = work.tile([P, R * PACK], BF16, name="fwi", tag="big", bufs=16, align_bytes=64)
            fwi.append(tl)
            nc.vector.tensor_tensor(
                out=tl[:].rearrange("p (m j t) -> p m j t", j=4, t=PACK),
                in0=fi[k][:].rearrange("p (j m t) -> p m j t", j=4, t=PACK),
                in1=w_sb[:, k, :].unsqueeze(1).unsqueeze(1).to_broadcast([P, P, 4, PACK]),
                op=ALU.mult,
            )

        f_interleave(0)
        f_interleave(1)
        f_weight(0)
        fq.append(quantize(fi[0][:], "f0"))
        f_weight(1)
        fwq.append(quantize(fwi[0][:], "fw0"))
        fq.append(quantize(fi[1][:], "f1"))
        fwq.append(quantize(fwi[1][:], "fw1"))

        bt = []
        bi = keep.tile([P, R * PACK], BF16, name="bi", align_bytes=64)
        GRAM_BANKS = ("pc", "pu", "pc", "pu")

        def gram(j):
            tl = psum.tile([P, PACK, P], F32, name=GRAM_BANKS[j], bufs=2)
            bt.append(tl)
            for t in range(PACK):
                for k in range(M_PASSES):
                    mx(tl[:, t, :], fq[k], slice(t * P, (t + 1) * P), fwq[k], slice(j * P, (j + 1) * P), k == 0, k == 1)

        def gram_out(j):
            nc.vector.tensor_tensor(
                out=bi[:, j * P * PACK : (j + 1) * P * PACK].rearrange("p (n t) -> p n t", t=PACK),
                in0=bt[j][:].rearrange("p t n -> p n t"),
                in1=qs[:].unsqueeze(1).to_broadcast([P, P, PACK]),
                op=ALU.mult,
            )

        mixed = [(u, 0) for u in range(PAIRS)] + list(PE_MIX)

        widen_some(4)
        x_mix(0, 0)
        widen_some(4)
        x_out(0, 0)
        x_mix(1, 0)
        g_transpose(0)
        widen_some(4)
        x_out(1, 0)
        x_mix(2, 0)
        widen_some(WIDEN_FIRST - 12)
        for j in range(4):
            gram(j)
        x_interleave(0, 1)
        x_interleave(1, 1)
        g_load_p(0)
        g_transpose(1)
        x_quantize(0, 0)
        gram_out(0)
        gram_out(1)
        x_quantize(0, 1)
        gram_out(2)
        g_quantize(0)
        gram_out(3)
        g_load_p(1)
        g_transpose(2)
        bq = quantize(bi[:], "b")
        x_quantize(1, 0)
        x_quantize(1, 1)
        g_quantize(1)

        pa, pc, pu = {}, {}, {}
        full = slice(0, R)

        def cols_of(i):
            return slice((i % 2) * P, (i % 2 + 1) * P)

        def products(u):
            for i in (2 * u, 2 * u + 1):
                tl = psum.tile([P, R], F32, name="pc", bufs=2)
                pc[i] = tl
                mx(tl[:], gpq[u], cols_of(i), bq, full, True, True)
            for i in (2 * u, 2 * u + 1):
                tl = psum.tile([P, R], F32, name="pa", bufs=2)
                pa[i] = tl
                for k in range(M_PASSES):
                    mx(tl[:], xq[u, k], cols_of(i), fwq[k], full, k == 0, k == M_PASSES - 1)
            for i in (2 * u, 2 * u + 1):
                tl = psum.tile([P, R], F32, name="pu", bufs=2)
                pu[i] = tl
                for k in range(M_PASSES):
                    mx(tl[:], xq[u, k], cols_of(i), fwq[k], full, k == 0, False)
                mx(tl[:], gpq[u], cols_of(i), bq, full, False, True)

        cneg, num, den = {}, {}, {}

        def parts(u):
            tl = work.tile([P, 2, R], F32, name="cneg", bufs=2)
            cneg[u] = tl
            for a in range(2):
                nc.scalar.activation(out=tl[:, a, :], in_=pc[2 * u + a][:], func=ACT.Relu, scale=-1.0)

        def sum_num(u):
            tl = work.tile([P, 2, R], F32, name="num", tag="big", bufs=16, align_bytes=64)
            num[u] = tl
            for a in range(2):
                nc.vector.scalar_tensor_tensor(
                    out=tl[:, a, :], in0=pa[2 * u + a][:], scalar=0.0, in1=cneg[u][:, a, :], op0=ALU.min, op1=ALU.subtract
                )

        def sum_den(u):
            tl = work.tile([P, 2, R], F32, name="den", tag="big", bufs=16, align_bytes=64)
            den[u] = tl
            for a in range(2):
                nc.vector.tensor_tensor(out=tl[:, a, :], in0=pu[2 * u + a][:], in1=num[u][:, a, :], op=ALU.subtract)

        def root(u, s):
            nc.scalar.activation(out=num[u][:, s, :], in_=num[u][:, s, :], func=ACT.Sqrt, scale=-1.0, bias=half[:])

        def inv_root(u, s):
            nc.scalar.activation(out=den[u][:, s, :], in_=den[u][:, s, :], func=ACT.Abs_reciprocal_sqrt, bias=half[:])

        ratio, res = {}, {}
        both = slice(0, 2)

        def ratios(u, s):
            if u not in ratio:
                tl = work.tile([P, 2, R], F32, name="ratio", bufs=2)
                ratio[u] = tl
            nc.vector.tensor_tensor(out=ratio[u][:, s, :], in0=num[u][:, s, :], in1=den[u][:, s, :], op=ALU.mult)

        def finish(u, s):
            if u not in res:
                tl = work.tile([P, 2, R], F32, name="res", bufs=3)
                res[u] = tl
            eng = nc.vector if u in VECTOR_FINISH else nc.gpsimd
            gs = g_sb[u // 2][:, 2 * (u % 2) : 2 * (u % 2) + 2, :]
            eng.tensor_tensor(out=res[u][:, s, :], in0=ratio[u][:, s, :], in1=gs[:, s, :], op=ALU.mult)
            nc.sync.dma_start(out=out_view[u][:, s, :], in_=res[u][:, s, :])

        fns = (root, inv_root)
        batch_of = {u: b for b, us in enumerate(BATCHES) for u in us}
        products(0)
        parts(0)
        queue = []
        for u in range(PAIRS):
            b = batch_of[u]
            v = u + 2
            prep = v < PAIRS
            ready = list(queue)
            queue.clear()
            sum_num(u)
            if prep:
                g_load_p(v)
            sum_den(u)
            if u + 1 < PAIRS:
                products(u + 1)
            if prep:
                x_out(v, 0)
            if v + 1 < PAIRS:
                x_mix(v + 1, 0)
                g_transpose(v + 1)
            if u + 1 < PAIRS:
                parts(u + 1)
            widen_some(WIDEN_EACH)
            fns[b % 2](u, both)
            if b > 0:
                prev, cur = BATCHES[b - 1], BATCHES[b]
                pos = cur.index(u)
                for j in prev[pos * len(prev) // len(cur) : (pos + 1) * len(prev) // len(cur)]:
                    fns[b % 2](j, both)
                    queue.append(j)
            if prep:
                if (v, 1) not in mixed:
                    x_interleave(v, 1)
                x_quantize(v, 0)
                x_quantize(v, 1)
                g_quantize(v)
            for j in ready:
                ratios(j, both)
                finish(j, both)
        for j in queue:
            ratios(j, both)
            finish(j, both)
        for j in BATCHES[-1]:
            for a in range(2):
                fns[len(BATCHES) % 2](j, slice(a, a + 1))
            for a in range(2):
                ratios(j, slice(a, a + 1))
            for a in range(2):
                finish(j, slice(a, a + 1))
